import numpy as np
import ml_dtypes


def mxq(x, axis, fmt="e4m3"):
    dtype, down = {"e4m3": (ml_dtypes.float8_e4m3fn, 7), "e5m2": (ml_dtypes.float8_e5m2, 14)}[fmt]
    v = np.moveaxis(np.asarray(x, np.float32).astype(ml_dtypes.bfloat16).astype(np.float64), axis, -1)
    blocks = v.reshape(v.shape[:-1] + (-1, 32))
    amax = np.abs(blocks).max(-1, keepdims=True)
    byte = np.maximum(np.where(amax > 0, np.frexp(amax)[1] - 1 + 127, 0) - down, 1)
    scale = np.exp2(byte - 127.0)
    codes = (blocks / scale).astype(np.float32).astype(dtype).astype(np.float64)
    return np.moveaxis((codes * scale).reshape(v.shape), -1, axis)


WIDE = False


def mx_kscale(k):
    if not WIDE:
        return np.ones(k)
    levels = np.array([10, -10, 5, -5, 0])
    if k % 512:
        return np.exp2(np.random.permutation(np.resize(levels, k // 32))).repeat(32)
    a = np.empty((k // 512, 16))
    for p in range(k // 512):
        a[p, :8] = np.random.permutation(np.resize(levels, 8))
        for g in range(8):
            far = levels[np.abs(levels - a[p, g]) >= 10]
            a[p, g + 8] = far[np.random.randint(len(far))]
    return np.exp2(a.ravel()).repeat(32)


BF16 = ml_dtypes.bfloat16


def bf(x):
    return np.asarray(x, np.float32).astype(BF16)


def f64(x):
    return np.asarray(x).astype(np.float64)


E2M1 = np.array([0.0, 0.5, 1.0, 1.5, 2.0, 3.0, 4.0, 6.0, -0.0, -0.5, -1.0, -1.5, -2.0, -3.0, -4.0, -6.0])


def pack_weight(w, fmt):
    k, n = w.shape
    w = f64(bf(w)).reshape(k // 32, 32, n)
    amax = np.abs(w).max(1)
    if fmt == "e4m3":
        byte = np.frexp(amax)[1] - 1 + 127 - 7
    else:
        mant, ex = np.frexp(amax / 6.0)
        byte = np.where(mant > 0.5, ex, ex - 1) + 127
    byte = np.clip(np.where(amax > 0, byte, 1), 1, 254)
    scaled = (w * np.exp2(127.0 - byte)[:, None, :]).reshape(k, n).astype(np.float32)
    by_word = np.ascontiguousarray(scaled.reshape(k // 512, 128, 4, n).transpose(0, 1, 3, 2))
    if fmt == "e4m3":
        words = by_word.astype(ml_dtypes.float8_e4m3fn).view(np.uint8)
    else:
        c = by_word.astype(ml_dtypes.float4_e2m1fn).view(np.uint8) & 0xF
        words = c[..., 0::2] | (c[..., 1::2] << 4)
    return np.ascontiguousarray(words), np.ascontiguousarray(byte.astype(np.uint8).reshape(k // 512, 16, n))


def unpack_weight(words, scales, fmt):
    g, p, n, _ = words.shape
    if fmt == "e4m3":
        vals = np.ascontiguousarray(words).view(ml_dtypes.float8_e4m3fn).astype(np.float64)
    else:
        nib = np.empty((g, p, n, 4), np.uint8)
        nib[..., 0::2] = words & 0xF
        nib[..., 1::2] = words >> 4
        vals = E2M1[nib]
    vals = vals * np.repeat(np.exp2(scales.astype(np.float64) - 127.0), 8, axis=1)[..., None]
    return vals.transpose(0, 1, 3, 2).reshape(g * 512, n)
def pack4(w):
    words, scales = pack_weight(w, "e2m1")
    return words.reshape(words.shape[0], 128, -1), scales


def unpack4(words, scales):
    return unpack_weight(words.reshape(words.shape[0], 128, -1, 2), scales, "e2m1")


C, P, L, G = 2048, 3072, 512, 1536


def setup_inputs():
    s = mx_kscale(P)
    t = mx_kscale(L)
    open_peaks = np.random.random((P, C)) < 0.5
    tfidf = np.log1p(8.0 * np.random.random((P, C)) * open_peaks)
    loadings = np.random.standard_normal((P, L)) / np.sqrt(P)
    readout = np.random.standard_normal((L, G)) / np.sqrt(L)
    x_words, x_scales = pack4(tfidf * s[:, None])
    v_words, v_scales = pack4(loadings / s[:, None] * t)
    w_words, w_scales = pack_weight(readout / t[:, None], "e4m3")
    return {"x_words": x_words, "x_scales": x_scales,
            "v_words": v_words, "v_scales": v_scales,
            "w_words": w_words, "w_scales": w_scales,
            "depth": bf(np.exp(0.3 * np.random.standard_normal(C))),
            "offset": bf(0.5 * np.random.standard_normal(L) * t),
            "bias": bf(0.3 * np.random.standard_normal(G))}


def reference(x_words, x_scales, v_words, v_scales, w_words, w_scales, depth, offset, bias):
    x = unpack4(x_words, x_scales)
    v = unpack4(v_words, v_scales)
    w = unpack_weight(w_words, w_scales, "e4m3")
    y = x.T @ v
    z = y * f64(depth)[:, None] + f64(offset)
    a = mxq(z, 1, "e4m3") @ w
    return np.maximum(a + f64(bias), 0.0)

@@ -1,0 +1,221 @@
+from contextlib import ExitStack
+
+import concourse.mybir as mybir
+from concourse.masks import make_identity
+
+CELLS, PEAKS, COMPS, GENES = 2048, 3072, 512, 1536
+FLOPS = 2 * CELLS * PEAKS * COMPS + 2 * CELLS * COMPS * GENES
+
+F32 = mybir.dt.float32
+BF16 = mybir.dt.bfloat16
+I32 = mybir.dt.int32
+U32 = mybir.dt.uint32
+U8 = mybir.dt.uint8
+FP8X4 = mybir.dt.float8_e4m3fn_x4
+FP4X4 = mybir.dt.float4_e2m1fn_x4
+ALU = mybir.AluOpType
+ACT = mybir.ActivationFunctionType
+
+P = 128
+PASSES = PEAKS // 512
+TILES = CELLS // P
+BANK = 512
+GENE_BANKS = GENES // BANK
+
+X_WORD_CHUNKS = ((0, 2), (2, 4), (4, 8), (8, 12), (12, 16))
+X_SCALE_CHUNKS = ((0, 4), (4, 8), (8, 16))
+V_SPLIT = 3
+GROUPS = ((0, 2), (2, 4), (4, 6), (6, 8), (8, 10), (10, 12), (12, 14), (14, 15), (15, 16))
+TURN_LAG = 2
+QUANT_LAG = 4
+READOUT_LAG = 17
+
+
+def tile_scatac_lsi_activity_s4_kernel(
+    tc, x_words, x_scales, v_words, v_scales, w_words, w_scales, depth, offset, bias, out
+):
+    nc = tc.nc
+    with ExitStack() as ctx:
+        keep = ctx.enter_context(tc.tile_pool(name="keep", bufs=1))
+        work = ctx.enter_context(tc.tile_pool(name="work", bufs=4))
+        psum = ctx.enter_context(tc.psum_pool(name="psum", bufs=1))
+        ctx.enter_context(tc.manual_schedule())
+
+        def plane_tile(engine, name, passes, cols):
+            plane = keep.tile([P, passes, cols], U8, name=name, align_bytes=64)
+            engine.memset(plane[:].rearrange("p g n -> p (g n)").bitcast(I32), 0)
+            return plane
+
+        def load_scale_row(queue, plane, scales, r, col0, col1):
+            rows = scales.bitcast(I32).rearrange("g (q r) n -> r q g n", r=4)
+            queue.dma_start(out=plane[r:P:32, :, :].bitcast(I32), in_=rows[r, :, :, col0 // 4 : col1 // 4])
+
+        x_rows = x_words.bitcast(I32).rearrange("g p n -> p g n")
+        v_rows = v_words.bitcast(I32).rearrange("g p n -> p g n")
+
+        def load_x_words(queue, chunk):
+            t0, t1 = X_WORD_CHUNKS[chunk]
+            words = keep.tile([P, PASSES, (t1 - t0) * P * 2], U8, name="xw%d" % chunk, align_bytes=64)
+            queue.dma_start(out=words[:].bitcast(I32), in_=x_rows[:, :, t0 * P // 2 : t1 * P // 2])
+            return words
+
+        def load_v_words(queue, g0, g1):
+            words = keep.tile([P, g1 - g0, COMPS * 2], U8, name="vw%d" % g0, align_bytes=64)
+            queue.dma_start(out=words[:].bitcast(I32), in_=v_rows[:, g0:g1, :])
+            return words
+
+        def x_plane_tile(engine, chunk):
+            t0, t1 = X_SCALE_CHUNKS[chunk]
+            return plane_tile(engine, "x_plane%d" % chunk, PASSES, (t1 - t0) * P)
+
+        def load_x_scale_row(queue, chunk, r):
+            t0, t1 = X_SCALE_CHUNKS[chunk]
+            load_scale_row(queue, xs[chunk], x_scales, r, t0 * P, t1 * P)
+
+        xw, xs = {}, {}
+        xw[0] = load_x_words(nc.sync, 0)
+        v_first = load_v_words(nc.scalar, 0, V_SPLIT)
+        v_plane = plane_tile(nc.vector, "v_plane", PASSES, COMPS)
+        xs[0] = x_plane_tile(nc.vector, 0)
+        w_plane = plane_tile(nc.vector, "w_plane", 1, GENES)
+        depth_rows = keep.tile([P, P], BF16, name="depth_rows")
+        nc.vector.memset(depth_rows[:], 0.0)
+        for r in range(4):
+            load_scale_row(nc.sync, v_plane, v_scales, r, 0, COMPS)
+        for r in range(2):
+            load_x_scale_row(nc.scalar, 0, r)
+        for r in range(2, 4):
+            load_x_scale_row(nc.gpsimd, 0, r)
+        nc.gpsimd.dma_start(out=depth_rows[0:TILES, :], in_=depth.rearrange("(t p) -> t p", p=P))
+        ident = keep.tile([P, P], F32, name="ident")
+        make_identity(nc, ident[:])
+        ident_bf = keep.tile([P, P], BF16, name="ident_bf")
+        nc.scalar.activation(out=ident_bf[:], in_=ident[:], func=ACT.Relu)
+        xs[1] = x_plane_tile(nc.gpsimd, 1)
+        xs[2] = x_plane_tile(nc.gpsimd, 2)
+
+        v_rest = load_v_words(nc.sync, V_SPLIT, PASSES)
+        offset_b = keep.tile([P, COMPS], BF16, name="offset_b")
+        nc.sync.dma_start(out=offset_b[:], in_=offset.partition_broadcast(P))
+        xw[1] = load_x_words(nc.sync, 1)
+        w_codes = keep.tile([P, GENES], U32, name="w_codes", align_bytes=64)
+        nc.sync.dma_start(out=w_codes[:].bitcast(I32), in_=w_words[0].rearrange("p n t -> p (n t)").bitcast(I32))
+        for r in range(4):
+            load_scale_row(nc.sync, w_plane, w_scales, r, 0, GENES)
+        bias_b = keep.tile([P, GENES], BF16, name="bias_b")
+        nc.sync.dma_start(out=bias_b[:], in_=bias.partition_broadcast(P))
+        xw[2] = load_x_words(nc.sync, 2)
+        for r in range(4):
+            load_x_scale_row(nc.sync, 1, r)
+        xw[3] = load_x_words(nc.sync, 3)
+        for r in range(4):
+            load_x_scale_row(nc.sync, 2, r)
+        xw[4] = load_x_words(nc.sync, 4)
+
+        depth_col = keep.tile([P, TILES], F32, name="depth_col")
+
+        def turn_depth():
+            depth_ps = psum.tile([P, P], BF16, name="depth_ps", tag="turn", bufs=1)
+            nc.tensor.transpose(depth_ps[:], depth_rows[:], ident_bf[:])
+            nc.scalar.copy(out=depth_col[:], in_=depth_ps[:, 0:TILES])
+
+        y_ps, z, zt, z_codes, z_scales, res = {}, {}, {}, {}, {}, {}
+
+        def chunk_of(chunks, i):
+            return [(c, i - t0) for c, (t0, t1) in enumerate(chunks) if t0 <= i < t1][0]
+
+        def project(i, g):
+            if g == 0:
+                y_ps[i] = psum.tile([P, COMPS], F32, name="y", tag="y", bufs=3)
+            wc, wi = chunk_of(X_WORD_CHUNKS, i)
+            sc, si = chunk_of(X_SCALE_CHUNKS, i)
+            v_g = v_first[:, g, :] if g < V_SPLIT else v_rest[:, g - V_SPLIT, :]
+            nc.tensor.matmul_mx(
+                out=y_ps[i][:],
+                lhsT=xw[wc][:, g, wi * P * 2 : (wi + 1) * P * 2].bitcast(FP4X4),
+                lhsT_scale=xs[sc][:, g, si * P : (si + 1) * P],
+                rhs=v_g.bitcast(FP4X4),
+                rhs_scale=v_plane[:, g, :],
+                start=(g == 0),
+                stop=(g == PASSES - 1),
+            )
+
+        def normalise(i):
+            z[i] = work.tile([P, 2, P, 2], BF16, name="z", tag="z")
+            y_view = y_ps[i][:].rearrange("p (q u e) -> p u q e", u=2, e=2)
+            o_view = offset_b[:].rearrange("p (q u e) -> p u q e", u=2, e=2)
+            for u in range(2):
+                nc.vector.scalar_tensor_tensor(
+                    out=z[i][:, u, :, :], in0=y_view[:, u, :, :], scalar=depth_col[:, i : i + 1],
+                    in1=o_view[:, u, :, :], op0=ALU.mult, op1=ALU.add,
+                )
+
+        def turn(t0, t1):
+            n = t1 - t0
+            turned = psum.tile([P, n, 2, P], F32, name="turned", tag="turn", bufs=1)
+            for i in range(t0, t1):
+                words = z[i][:].rearrange("p u q e -> p (u q e)").bitcast(F32)
+                for u in range(2):
+                    nc.tensor.transpose(turned[:, i - t0, u, :], words[:, u * P : (u + 1) * P], ident[:])
+            zt[t0] = work.tile([P, n * P * 4], BF16, name="zt", tag="zt", align_bytes=64)
+            nc.scalar.copy(
+                out=zt[t0][:].bitcast(F32).rearrange("p (i c u) -> p i c u", i=n, u=2),
+                in_=turned[:].rearrange("p i u c -> p i c u"),
+            )
+
+        def quantise(t0, t1):
+            n = t1 - t0
+            codes = work.tile([P, n * P], U32, name="codes", tag="codes", align_bytes=64)
+            scales = work.tile([P, n * P], U8, name="scales", tag="scales", align_bytes=64)
+            nc.vector.quantize_mx(out=codes[:].bitcast(FP8X4), scales=scales[:], in_=zt[t0][:])
+            for i in range(t0, t1):
+                z_codes[i] = codes[:, (i - t0) * P : (i - t0 + 1) * P]
+                z_scales[i] = scales[:, (i - t0) * P : (i - t0 + 1) * P]
+
+        def read_out(m):
+            i, b = divmod(m, GENE_BANKS)
+            cols = slice(b * BANK, (b + 1) * BANK)
+            if b == 0:
+                res[i] = work.tile([P, GENES], F32, name="res", tag="res", bufs=8)
+            a_ps = psum.tile([P, BANK], F32, name="a", tag="a", bufs=4)
+            nc.tensor.matmul_mx(
+                out=a_ps[:],
+                lhsT=z_codes[i].bitcast(FP8X4),
+                lhsT_scale=z_scales[i],
+                rhs=w_codes[:, cols].bitcast(FP8X4),
+                rhs_scale=w_plane[:, 0, cols],
+                start=True,
+                stop=True,
+            )
+            nc.vector.tensor_tensor(out=res[i][:, cols], in0=a_ps[:], in1=bias_b[:, cols], op=ALU.add)
+
+        def finish(m):
+            i, b = divmod(m, GENE_BANKS)
+            cols = slice(b * BANK, (b + 1) * BANK)
+            nc.scalar.activation(out=res[i][:, cols], in_=res[i][:, cols], func=ACT.Relu)
+            rows = slice(i * P, (i + 1) * P)
+            if i >= TILES - 2:
+                nc.sync.dma_start(out=out[rows, cols], in_=res[i][:, cols])
+            elif b == GENE_BANKS - 1:
+                nc.sync.dma_start(out=out[rows, :], in_=res[i][:])
+
+        group_ending_at = {t1 * PASSES - 1: (t0, t1) for t0, t1 in GROUPS}
+        readouts = TILES * GENE_BANKS
+        for n in range(READOUT_LAG + 2 * readouts + 1):
+            if n < TILES * PASSES:
+                i, g = divmod(n, PASSES)
+                project(i, g)
+                if n == V_SPLIT - 1:
+                    turn_depth()
+                if g == PASSES - 1:
+                    normalise(i)
+            if n - TURN_LAG in group_ending_at:
+                turn(*group_ending_at[n - TURN_LAG])
+            if n - QUANT_LAG in group_ending_at:
+                quantise(*group_ending_at[n - QUANT_LAG])
+            m, odd = divmod(n - READOUT_LAG, 2)
+            if odd == 0 and 0 <= m:
+                if m < readouts:
+                    read_out(m)
+                if m >= 1:
+                    finish(m - 1)

@@ -25,6 +25,9 @@ GENE_BANKS = GENES // BANK
 X_WORD_CHUNKS = ((0, 2), (2, 4), (4, 8), (8, 12), (12, 16))
 X_SCALE_CHUNKS = ((0, 4), (4, 8), (8, 16))
 V_SPLIT = 3
+OFFSET_ROWS = COMPS // (2 * P)
+WORD_ROWS = OFFSET_ROWS + GENES // (2 * P)
+DEPTH_ROW0 = 32
 GROUPS = ((0, 2), (2, 4), (4, 6), (6, 8), (8, 10), (10, 12), (12, 14), (14, 15), (15, 16))
 TURN_LAG = 2
 QUANT_LAG = 4
@@ -73,37 +76,33 @@ def tile_scatac_lsi_activity_s4_kernel(
             load_scale_row(queue, xs[chunk], x_scales, r, t0 * P, t1 * P)
 
         xw, xs = {}, {}
-        xw[0] = load_x_words(nc.sync, 0)
-        v_first = load_v_words(nc.scalar, 0, V_SPLIT)
+        ident = keep.tile([P, P], F32, name="ident")
+        make_identity(nc, ident[:])
+        vec_rows = keep.tile([P, 2 * P], BF16, name="vec_rows")
+        nc.vector.memset(vec_rows[:], 0.0)
         v_plane = plane_tile(nc.vector, "v_plane", PASSES, COMPS)
         xs[0] = x_plane_tile(nc.vector, 0)
         w_plane = plane_tile(nc.vector, "w_plane", 1, GENES)
-        depth_rows = keep.tile([P, P], BF16, name="depth_rows")
-        nc.vector.memset(depth_rows[:], 0.0)
+        xs[1] = x_plane_tile(nc.vector, 1)
+        xs[2] = x_plane_tile(nc.vector, 2)
+
+        nc.sync.dma_start(out=vec_rows[0:OFFSET_ROWS, :], in_=offset.rearrange("(r n) -> r n", n=2 * P))
+        nc.sync.dma_start(out=vec_rows[DEPTH_ROW0 : DEPTH_ROW0 + TILES, 0:P], in_=depth.rearrange("(t p) -> t p", p=P))
+        nc.sync.dma_start(out=vec_rows[OFFSET_ROWS:WORD_ROWS, :], in_=bias.rearrange("(r n) -> r n", n=2 * P))
+        xw[0] = load_x_words(nc.scalar, 0)
         for r in range(4):
             load_scale_row(nc.sync, v_plane, v_scales, r, 0, COMPS)
-        for r in range(2):
-            load_x_scale_row(nc.scalar, 0, r)
-        for r in range(2, 4):
-            load_x_scale_row(nc.gpsimd, 0, r)
-        nc.gpsimd.dma_start(out=depth_rows[0:TILES, :], in_=depth.rearrange("(t p) -> t p", p=P))
-        ident = keep.tile([P, P], F32, name="ident")
-        make_identity(nc, ident[:])
         ident_bf = keep.tile([P, P], BF16, name="ident_bf")
         nc.scalar.activation(out=ident_bf[:], in_=ident[:], func=ACT.Relu)
-        xs[1] = x_plane_tile(nc.gpsimd, 1)
-        xs[2] = x_plane_tile(nc.gpsimd, 2)
-
+        v_first = load_v_words(nc.sync, 0, V_SPLIT)
+        for r in range(4):
+            load_x_scale_row(nc.sync, 0, r)
         v_rest = load_v_words(nc.sync, V_SPLIT, PASSES)
-        offset_b = keep.tile([P, COMPS], BF16, name="offset_b")
-        nc.sync.dma_start(out=offset_b[:], in_=offset.partition_broadcast(P))
         xw[1] = load_x_words(nc.sync, 1)
         w_codes = keep.tile([P, GENES], U32, name="w_codes", align_bytes=64)
         nc.sync.dma_start(out=w_codes[:].bitcast(I32), in_=w_words[0].rearrange("p n t -> p (n t)").bitcast(I32))
         for r in range(4):
             load_scale_row(nc.sync, w_plane, w_scales, r, 0, GENES)
-        bias_b = keep.tile([P, GENES], BF16, name="bias_b")
-        nc.sync.dma_start(out=bias_b[:], in_=bias.partition_broadcast(P))
         xw[2] = load_x_words(nc.sync, 2)
         for r in range(4):
             load_x_scale_row(nc.sync, 1, r)
@@ -113,11 +112,33 @@ def tile_scatac_lsi_activity_s4_kernel(
         xw[4] = load_x_words(nc.sync, 4)
 
         depth_col = keep.tile([P, TILES], F32, name="depth_col")
+        word_cols = keep.tile([P, WORD_ROWS], F32, name="word_cols")
+        cols_ps = psum.tile([P, P], F32, name="cols_ps", tag="turn", bufs=1)
+        nc.tensor.transpose(cols_ps[:], vec_rows[:].bitcast(F32), ident[:])
+        nc.scalar.copy(out=word_cols[:], in_=cols_ps[:, 0:WORD_ROWS])
+        depth_ps = psum.tile([P, P], BF16, name="depth_ps", tag="y", bufs=3)
+        nc.tensor.transpose(depth_ps[:], vec_rows[:, 0:P], ident_bf[:])
+        nc.vector.tensor_copy(out=depth_col[:], in_=depth_ps[:, DEPTH_ROW0 : DEPTH_ROW0 + TILES])
 
-        def turn_depth():
-            depth_ps = psum.tile([P, P], BF16, name="depth_ps", tag="turn", bufs=1)
-            nc.tensor.transpose(depth_ps[:], depth_rows[:], ident_bf[:])
-            nc.scalar.copy(out=depth_col[:], in_=depth_ps[:, 0:TILES])
+        def spread(row0, row1):
+            spread_ps = psum.tile([P, (row1 - row0) * P], F32, name="spread_ps", tag="a", bufs=4)
+            for r in range(row0, row1):
+                nc.tensor.transpose(
+                    spread_ps[:, (r - row0) * P : (r - row0 + 1) * P],
+                    word_cols[:, r : r + 1].to_broadcast([P, P]), ident[:],
+                )
+            return spread_ps
+
+        offset_b = keep.tile([P, 2, P, 2], BF16, name="offset_b")
+        bias_b = keep.tile([P, GENES], BF16, name="bias_b")
+        nc.vector.tensor_copy(
+            out=offset_b[:].rearrange("p u q e -> p (u q e)").bitcast(F32).rearrange("p (u q) -> p u q", u=2),
+            in_=spread(0, OFFSET_ROWS)[:].rearrange("p (q u) -> p u q", u=2),
+        )
+        bias_words = bias_b[:].bitcast(F32)
+        half = (WORD_ROWS - OFFSET_ROWS) // 2
+        nc.scalar.copy(out=bias_words[:, 0 : half * P], in_=spread(OFFSET_ROWS, OFFSET_ROWS + half)[:])
+        nc.vector.tensor_copy(out=bias_words[:, half * P :], in_=spread(OFFSET_ROWS + half, WORD_ROWS)[:])
 
         y_ps, z, zt, z_codes, z_scales, res = {}, {}, {}, {}, {}, {}
 
@@ -143,11 +164,10 @@ def tile_scatac_lsi_activity_s4_kernel(
         def normalise(i):
             z[i] = work.tile([P, 2, P, 2], BF16, name="z", tag="z")
             y_view = y_ps[i][:].rearrange("p (q u e) -> p u q e", u=2, e=2)
-            o_view = offset_b[:].rearrange("p (q u e) -> p u q e", u=2, e=2)
             for u in range(2):
                 nc.vector.scalar_tensor_tensor(
                     out=z[i][:, u, :, :], in0=y_view[:, u, :, :], scalar=depth_col[:, i : i + 1],
-                    in1=o_view[:, u, :, :], op0=ALU.mult, op1=ALU.add,
+                    in1=offset_b[:, u, :, :], op0=ALU.mult, op1=ALU.add,
                 )
 
         def turn(t0, t1):
@@ -205,8 +225,6 @@ def tile_scatac_lsi_activity_s4_kernel(
             if n < TILES * PASSES:
                 i, g = divmod(n, PASSES)
                 project(i, g)
-                if n == V_SPLIT - 1:
-                    turn_depth()
                 if g == PASSES - 1:
                     normalise(i)
             if n - TURN_LAG in group_ending_at:

@@ -26,12 +26,10 @@ X_WORD_CHUNKS = ((0, 2), (2, 4), (4, 8), (8, 12), (12, 16))
 X_SCALE_CHUNKS = ((0, 4), (4, 8), (8, 16))
 V_SPLIT = 3
 OFFSET_ROWS = COMPS // (2 * P)
-WORD_ROWS = OFFSET_ROWS + GENES // (2 * P)
+BIAS_ROWS = 8
+BIAS_ROW_WORDS = GENES // (2 * BIAS_ROWS)
+WORD_ROWS = OFFSET_ROWS + BIAS_ROWS
 DEPTH_ROW0 = 32
-GROUPS = ((0, 2), (2, 4), (4, 6), (6, 8), (8, 10), (10, 12), (12, 14), (14, 15), (15, 16))
-TURN_LAG = 2
-QUANT_LAG = 4
-READOUT_LAG = 17
 
 
 def tile_scatac_lsi_activity_s4_kernel(
@@ -88,7 +86,9 @@ def tile_scatac_lsi_activity_s4_kernel(
 
         nc.sync.dma_start(out=vec_rows[0:OFFSET_ROWS, :], in_=offset.rearrange("(r n) -> r n", n=2 * P))
         nc.sync.dma_start(out=vec_rows[DEPTH_ROW0 : DEPTH_ROW0 + TILES, 0:P], in_=depth.rearrange("(t p) -> t p", p=P))
-        nc.sync.dma_start(out=vec_rows[OFFSET_ROWS:WORD_ROWS, :], in_=bias.rearrange("(r n) -> r n", n=2 * P))
+        nc.sync.dma_start(
+            out=vec_rows[OFFSET_ROWS:WORD_ROWS, 0 : 2 * BIAS_ROW_WORDS], in_=bias.rearrange("(r n) -> r n", r=BIAS_ROWS)
+        )
         xw[0] = load_x_words(nc.scalar, 0)
         for r in range(4):
             load_scale_row(nc.sync, v_plane, v_scales, r, 0, COMPS)
@@ -113,15 +113,15 @@ def tile_scatac_lsi_activity_s4_kernel(
 
         depth_col = keep.tile([P, TILES], F32, name="depth_col")
         word_cols = keep.tile([P, WORD_ROWS], F32, name="word_cols")
-        cols_ps = psum.tile([P, P], F32, name="cols_ps", tag="turn", bufs=1)
+        cols_ps = psum.tile([P, P], F32, name="cols_ps", tag="y", bufs=2)
         nc.tensor.transpose(cols_ps[:], vec_rows[:].bitcast(F32), ident[:])
         nc.scalar.copy(out=word_cols[:], in_=cols_ps[:, 0:WORD_ROWS])
-        depth_ps = psum.tile([P, P], BF16, name="depth_ps", tag="y", bufs=3)
+        depth_ps = psum.tile([P, P], BF16, name="depth_ps", tag="y", bufs=2)
         nc.tensor.transpose(depth_ps[:], vec_rows[:, 0:P], ident_bf[:])
         nc.vector.tensor_copy(out=depth_col[:], in_=depth_ps[:, DEPTH_ROW0 : DEPTH_ROW0 + TILES])
 
         def spread(row0, row1):
-            spread_ps = psum.tile([P, (row1 - row0) * P], F32, name="spread_ps", tag="a", bufs=4)
+            spread_ps = psum.tile([P, (row1 - row0) * P], F32, name="spread_ps", tag="a", bufs=6)
             for r in range(row0, row1):
                 nc.tensor.transpose(
                     spread_ps[:, (r - row0) * P : (r - row0 + 1) * P],
@@ -135,19 +135,23 @@ def tile_scatac_lsi_activity_s4_kernel(
             out=offset_b[:].rearrange("p u q e -> p (u q e)").bitcast(F32).rearrange("p (u q) -> p u q", u=2),
             in_=spread(0, OFFSET_ROWS)[:].rearrange("p (q u) -> p u q", u=2),
         )
-        bias_words = bias_b[:].bitcast(F32)
-        half = (WORD_ROWS - OFFSET_ROWS) // 2
-        nc.scalar.copy(out=bias_words[:, 0 : half * P], in_=spread(OFFSET_ROWS, OFFSET_ROWS + half)[:])
-        nc.vector.tensor_copy(out=bias_words[:, half * P :], in_=spread(OFFSET_ROWS + half, WORD_ROWS)[:])
+        bias_words = bias_b[:].bitcast(F32).rearrange("p (r n) -> p r n", r=BIAS_ROWS)
+        half = BIAS_ROWS // 2
+        for h, copy in enumerate((nc.scalar.copy, nc.vector.tensor_copy)):
+            rows_ps = spread(OFFSET_ROWS + h * half, OFFSET_ROWS + (h + 1) * half)
+            copy(
+                out=bias_words[:, h * half : (h + 1) * half, :],
+                in_=rows_ps[:].rearrange("p (r n) -> p r n", r=half)[:, :, 0:BIAS_ROW_WORDS],
+            )
 
-        y_ps, z, zt, z_codes, z_scales, res = {}, {}, {}, {}, {}, {}
+        y_ps, z, zt, z_codes, z_scales, res, a_ps = {}, {}, {}, {}, {}, {}, {}
 
         def chunk_of(chunks, i):
             return [(c, i - t0) for c, (t0, t1) in enumerate(chunks) if t0 <= i < t1][0]
 
         def project(i, g):
             if g == 0:
-                y_ps[i] = psum.tile([P, COMPS], F32, name="y", tag="y", bufs=3)
+                y_ps[i] = psum.tile([P, COMPS], F32, name="y", tag="y", bufs=2)
             wc, wi = chunk_of(X_WORD_CHUNKS, i)
             sc, si = chunk_of(X_SCALE_CHUNKS, i)
             v_g = v_first[:, g, :] if g < V_SPLIT else v_rest[:, g - V_SPLIT, :]
@@ -172,7 +176,7 @@ def tile_scatac_lsi_activity_s4_kernel(
 
         def turn(t0, t1):
             n = t1 - t0
-            turned = psum.tile([P, n, 2, P], F32, name="turned", tag="turn", bufs=1)
+            turned = psum.tile([P, n, 2, P], F32, name="turned", tag="y", bufs=2)
             for i in range(t0, t1):
                 words = z[i][:].rearrange("p u q e -> p (u q e)").bitcast(F32)
                 for u in range(2):
@@ -192,48 +196,66 @@ def tile_scatac_lsi_activity_s4_kernel(
                 z_codes[i] = codes[:, (i - t0) * P : (i - t0 + 1) * P]
                 z_scales[i] = scales[:, (i - t0) * P : (i - t0 + 1) * P]
 
-        def read_out(m):
-            i, b = divmod(m, GENE_BANKS)
-            cols = slice(b * BANK, (b + 1) * BANK)
-            if b == 0:
-                res[i] = work.tile([P, GENES], F32, name="res", tag="res", bufs=8)
-            a_ps = psum.tile([P, BANK], F32, name="a", tag="a", bufs=4)
-            nc.tensor.matmul_mx(
-                out=a_ps[:],
-                lhsT=z_codes[i].bitcast(FP8X4),
-                lhsT_scale=z_scales[i],
-                rhs=w_codes[:, cols].bitcast(FP8X4),
-                rhs_scale=w_plane[:, 0, cols],
-                start=True,
-                stop=True,
-            )
-            nc.vector.tensor_tensor(out=res[i][:, cols], in0=a_ps[:], in1=bias_b[:, cols], op=ALU.add)
+        def read_out(i):
+            res[i] = work.tile([P, GENES], F32, name="res", tag="res", bufs=8)
+            for b in range(GENE_BANKS):
+                cols = slice(b * BANK, (b + 1) * BANK)
+                a_ps[i, b] = psum.tile([P, BANK], F32, name="a", tag="a", bufs=6)
+                nc.tensor.matmul_mx(
+                    out=a_ps[i, b][:],
+                    lhsT=z_codes[i].bitcast(FP8X4),
+                    lhsT_scale=z_scales[i],
+                    rhs=w_codes[:, cols].bitcast(FP8X4),
+                    rhs_scale=w_plane[:, 0, cols],
+                    start=True,
+                    stop=True,
+                )
 
-        def finish(m):
-            i, b = divmod(m, GENE_BANKS)
-            cols = slice(b * BANK, (b + 1) * BANK)
-            nc.scalar.activation(out=res[i][:, cols], in_=res[i][:, cols], func=ACT.Relu)
+        def finish(i, b):
             rows = slice(i * P, (i + 1) * P)
-            if i >= TILES - 2:
-                nc.sync.dma_start(out=out[rows, cols], in_=res[i][:, cols])
-            elif b == GENE_BANKS - 1:
+            width = BANK // 2 if (i, b) == (TILES - 1, GENE_BANKS - 1) else BANK
+            for c0 in range(0, BANK, width):
+                cols = slice(b * BANK + c0, b * BANK + c0 + width)
+                nc.vector.tensor_tensor(
+                    out=res[i][:, cols], in0=a_ps[i, b][:, c0 : c0 + width], in1=bias_b[:, cols], op=ALU.add
+                )
+                nc.scalar.activation(out=res[i][:, cols], in_=res[i][:, cols], func=ACT.Relu)
+                if i >= TILES - 2:
+                    nc.sync.dma_start(out=out[rows, cols], in_=res[i][:, cols])
+            if i < TILES - 2 and b == GENE_BANKS - 1:
                 nc.sync.dma_start(out=out[rows, :], in_=res[i][:])
 
-        group_ending_at = {t1 * PASSES - 1: (t0, t1) for t0, t1 in GROUPS}
-        readouts = TILES * GENE_BANKS
-        for n in range(READOUT_LAG + 2 * readouts + 1):
-            if n < TILES * PASSES:
-                i, g = divmod(n, PASSES)
+        def project_tile(i):
+            for g in range(PASSES):
                 project(i, g)
-                if g == PASSES - 1:
-                    normalise(i)
-            if n - TURN_LAG in group_ending_at:
-                turn(*group_ending_at[n - TURN_LAG])
-            if n - QUANT_LAG in group_ending_at:
-                quantise(*group_ending_at[n - QUANT_LAG])
-            m, odd = divmod(n - READOUT_LAG, 2)
-            if odd == 0 and 0 <= m:
-                if m < readouts:
-                    read_out(m)
-                if m >= 1:
-                    finish(m - 1)
+                if i == 2 and g == GENE_BANKS - 1:
+                    turn(0, 2)
+                    quantise(0, 2)
+            normalise(i)
+
+        def read_out_round(tiles, group, before_turn, before_quantise):
+            banks = [(i, b) for i in tiles for b in range(GENE_BANKS)]
+            for i in tiles:
+                read_out(i)
+            for i, b in banks[:before_turn]:
+                finish(i, b)
+            turn(*group)
+            for i, b in banks[before_turn:before_quantise]:
+                finish(i, b)
+            quantise(*group)
+            for i, b in banks[before_quantise:]:
+                finish(i, b)
+
+        project_tile(0)
+        project_tile(1)
+        for t in range(2, TILES - 2, 2):
+            project_tile(t)
+            project_tile(t + 1)
+            read_out_round((t - 2, t - 1), (t, t + 2), 2, 4)
+        for t in range(TILES - 2, TILES):
+            project_tile(t)
+            read_out_round((t - 2,), (t, t + 1), 0, 2)
+        for t in range(TILES - 2, TILES):
+            read_out(t)
+            for b in range(GENE_BANKS):
+                finish(t, b)

@@ -23,8 +23,9 @@ BANK = 512
 GENE_BANKS = GENES // BANK
 
 X_WORD_CHUNKS = ((0, 2), (2, 4), (4, 8), (8, 12), (12, 16))
-X_SCALE_CHUNKS = ((0, 4), (4, 8), (8, 16))
-V_SPLIT = 3
+X_SCALE_CHUNKS = ((0, 2), (2, 6), (6, 16))
+V_WORD_CHUNKS = ((0, 1), (1, 3), (3, 6))
+HALF = PASSES // 2
 OFFSET_ROWS = COMPS // (2 * P)
 BIAS_ROWS = 8
 BIAS_ROW_WORDS = GENES // (2 * BIAS_ROWS)
@@ -54,16 +55,19 @@ def tile_scatac_lsi_activity_s4_kernel(
         x_rows = x_words.bitcast(I32).rearrange("g p n -> p g n")
         v_rows = v_words.bitcast(I32).rearrange("g p n -> p g n")
 
-        def load_x_words(queue, chunk):
+        def load_x_words(queue, chunk, g0=0, g1=PASSES):
             t0, t1 = X_WORD_CHUNKS[chunk]
-            words = keep.tile([P, PASSES, (t1 - t0) * P * 2], U8, name="xw%d" % chunk, align_bytes=64)
-            queue.dma_start(out=words[:].bitcast(I32), in_=x_rows[:, :, t0 * P // 2 : t1 * P // 2])
-            return words
+            words = keep.tile([P, g1 - g0, (t1 - t0) * P * 2], U8, name="xw%d_%d" % (chunk, g0), align_bytes=64)
+            queue.dma_start(out=words[:].bitcast(I32), in_=x_rows[:, g0:g1, t0 * P // 2 : t1 * P // 2])
+            for g in range(g0, g1):
+                xw[chunk, g] = words[:, g - g0, :]
 
-        def load_v_words(queue, g0, g1):
-            words = keep.tile([P, g1 - g0, COMPS * 2], U8, name="vw%d" % g0, align_bytes=64)
-            queue.dma_start(out=words[:].bitcast(I32), in_=v_rows[:, g0:g1, :])
-            return words
+        def load_v_words(chunk):
+            g0, g1 = V_WORD_CHUNKS[chunk]
+            words = keep.tile([P, g1 - g0, COMPS * 2], U8, name="vw%d" % chunk, align_bytes=64)
+            nc.sync.dma_start(out=words[:].bitcast(I32), in_=v_rows[:, g0:g1, :])
+            for g in range(g0, g1):
+                vw[g] = words[:, g - g0, :]
 
         def x_plane_tile(engine, chunk):
             t0, t1 = X_SCALE_CHUNKS[chunk]
@@ -73,15 +77,15 @@ def tile_scatac_lsi_activity_s4_kernel(
             t0, t1 = X_SCALE_CHUNKS[chunk]
             load_scale_row(queue, xs[chunk], x_scales, r, t0 * P, t1 * P)
 
-        xw, xs = {}, {}
+        xw, xs, vw = {}, {}, {}
         ident = keep.tile([P, P], F32, name="ident")
         make_identity(nc, ident[:])
         vec_rows = keep.tile([P, 2 * P], BF16, name="vec_rows")
         nc.vector.memset(vec_rows[:], 0.0)
         v_plane = plane_tile(nc.vector, "v_plane", PASSES, COMPS)
         xs[0] = x_plane_tile(nc.vector, 0)
-        w_plane = plane_tile(nc.vector, "w_plane", 1, GENES)
         xs[1] = x_plane_tile(nc.vector, 1)
+        w_plane = plane_tile(nc.vector, "w_plane", 1, GENES)
         xs[2] = x_plane_tile(nc.vector, 2)
 
         nc.sync.dma_start(out=vec_rows[0:OFFSET_ROWS, :], in_=offset.rearrange("(r n) -> r n", n=2 * P))
@@ -89,27 +93,29 @@ def tile_scatac_lsi_activity_s4_kernel(
         nc.sync.dma_start(
             out=vec_rows[OFFSET_ROWS:WORD_ROWS, 0 : 2 * BIAS_ROW_WORDS], in_=bias.rearrange("(r n) -> r n", r=BIAS_ROWS)
         )
-        xw[0] = load_x_words(nc.scalar, 0)
+        load_x_words(nc.scalar, 0, 0, HALF)
         for r in range(4):
             load_scale_row(nc.sync, v_plane, v_scales, r, 0, COMPS)
         ident_bf = keep.tile([P, P], BF16, name="ident_bf")
         nc.scalar.activation(out=ident_bf[:], in_=ident[:], func=ACT.Relu)
-        v_first = load_v_words(nc.sync, 0, V_SPLIT)
+        load_v_words(0)
         for r in range(4):
             load_x_scale_row(nc.sync, 0, r)
-        v_rest = load_v_words(nc.sync, V_SPLIT, PASSES)
-        xw[1] = load_x_words(nc.sync, 1)
+        load_v_words(1)
+        load_x_words(nc.sync, 0, HALF, PASSES)
+        load_v_words(2)
+        load_x_words(nc.sync, 1)
+        for r in range(4):
+            load_x_scale_row(nc.sync, 1, r)
         w_codes = keep.tile([P, GENES], U32, name="w_codes", align_bytes=64)
         nc.sync.dma_start(out=w_codes[:].bitcast(I32), in_=w_words[0].rearrange("p n t -> p (n t)").bitcast(I32))
         for r in range(4):
             load_scale_row(nc.sync, w_plane, w_scales, r, 0, GENES)
-        xw[2] = load_x_words(nc.sync, 2)
-        for r in range(4):
-            load_x_scale_row(nc.sync, 1, r)
-        xw[3] = load_x_words(nc.sync, 3)
+        load_x_words(nc.sync, 2)
         for r in range(4):
             load_x_scale_row(nc.sync, 2, r)
-        xw[4] = load_x_words(nc.sync, 4)
+        load_x_words(nc.sync, 3)
+        load_x_words(nc.sync, 4)
 
         depth_col = keep.tile([P, TILES], F32, name="depth_col")
         word_cols = keep.tile([P, WORD_ROWS], F32, name="word_cols")
@@ -154,12 +160,11 @@ def tile_scatac_lsi_activity_s4_kernel(
                 y_ps[i] = psum.tile([P, COMPS], F32, name="y", tag="y", bufs=2)
             wc, wi = chunk_of(X_WORD_CHUNKS, i)
             sc, si = chunk_of(X_SCALE_CHUNKS, i)
-            v_g = v_first[:, g, :] if g < V_SPLIT else v_rest[:, g - V_SPLIT, :]
             nc.tensor.matmul_mx(
                 out=y_ps[i][:],
-                lhsT=xw[wc][:, g, wi * P * 2 : (wi + 1) * P * 2].bitcast(FP4X4),
+                lhsT=xw[wc, g][:, wi * P * 2 : (wi + 1) * P * 2].bitcast(FP4X4),
                 lhsT_scale=xs[sc][:, g, si * P : (si + 1) * P],
-                rhs=v_g.bitcast(FP4X4),
+                rhs=vw[g].bitcast(FP4X4),
                 rhs_scale=v_plane[:, g, :],
                 start=(g == 0),
                 stop=(g == PASSES - 1),
@@ -213,17 +218,26 @@ def tile_scatac_lsi_activity_s4_kernel(
 
         def finish(i, b):
             rows = slice(i * P, (i + 1) * P)
-            width = BANK // 2 if (i, b) == (TILES - 1, GENE_BANKS - 1) else BANK
-            for c0 in range(0, BANK, width):
-                cols = slice(b * BANK + c0, b * BANK + c0 + width)
-                nc.vector.tensor_tensor(
-                    out=res[i][:, cols], in0=a_ps[i, b][:, c0 : c0 + width], in1=bias_b[:, cols], op=ALU.add
-                )
-                nc.scalar.activation(out=res[i][:, cols], in_=res[i][:, cols], func=ACT.Relu)
-                if i >= TILES - 2:
-                    nc.sync.dma_start(out=out[rows, cols], in_=res[i][:, cols])
-            if i < TILES - 2 and b == GENE_BANKS - 1:
+            cols = slice(b * BANK, (b + 1) * BANK)
+            nc.vector.tensor_tensor(out=res[i][:, cols], in0=a_ps[i, b][:], in1=bias_b[:, cols], op=ALU.add)
+            nc.scalar.activation(out=res[i][:, cols], in_=res[i][:, cols], func=ACT.Relu)
+            if i >= TILES - 3:
+                nc.sync.dma_start(out=out[rows, cols], in_=res[i][:, cols])
+            elif b == GENE_BANKS - 1:
                 nc.sync.dma_start(out=out[rows, :], in_=res[i][:])
+
+        def finish_last_bank():
+            i, b = TILES - 1, GENE_BANKS - 1
+            halves = [slice(c0, c0 + BANK // 2) for c0 in (0, BANK // 2)]
+            last = res[i][:, b * BANK :]
+            for half_cols in halves:
+                nc.vector.tensor_tensor(
+                    out=last[:, half_cols], in0=a_ps[i, b][:, half_cols],
+                    in1=bias_b[:, b * BANK :][:, half_cols], op=ALU.add,
+                )
+            for half_cols in halves:
+                nc.vector.tensor_scalar_max(out=last[:, half_cols], in0=last[:, half_cols], scalar1=0.0)
+                nc.sync.dma_start(out=out[i * P :, b * BANK :][:, half_cols], in_=last[:, half_cols])
 
         def project_tile(i):
             for g in range(PASSES):
@@ -246,16 +260,23 @@ def tile_scatac_lsi_activity_s4_kernel(
             for i, b in banks[before_quantise:]:
                 finish(i, b)
 
-        project_tile(0)
-        project_tile(1)
-        for t in range(2, TILES - 2, 2):
+        for g in range(HALF):
+            project(0, g)
+            project(1, g)
+        for i in range(2):
+            for g in range(HALF, PASSES):
+                project(i, g)
+            normalise(i)
+        for t in range(2, TILES - 4, 2):
             project_tile(t)
             project_tile(t + 1)
             read_out_round((t - 2, t - 1), (t, t + 2), 2, 4)
-        for t in range(TILES - 2, TILES):
+        project_tile(TILES - 4)
+        read_out_round((TILES - 6, TILES - 5), (TILES - 4, TILES - 3), 2, 4)
+        for t in range(TILES - 3, TILES):
             project_tile(t)
-            read_out_round((t - 2,), (t, t + 1), 0, 2)
-        for t in range(TILES - 2, TILES):
-            read_out(t)
-            for b in range(GENE_BANKS):
-                finish(t, b)
+            read_out_round((t - 1,), (t, t + 1), 0, 2)
+        read_out(TILES - 1)
+        for b in range(GENE_BANKS - 1):
+            finish(TILES - 1, b)
+        finish_last_bank()

from contextlib import ExitStack

import concourse.mybir as mybir
from concourse.masks import make_identity

CELLS, PEAKS, COMPS, GENES = 2048, 3072, 512, 1536
FLOPS = 2 * CELLS * PEAKS * COMPS + 2 * CELLS * COMPS * GENES

F32 = mybir.dt.float32
BF16 = mybir.dt.bfloat16
I32 = mybir.dt.int32
U32 = mybir.dt.uint32
U8 = mybir.dt.uint8
FP8X4 = mybir.dt.float8_e4m3fn_x4
FP4X4 = mybir.dt.float4_e2m1fn_x4
ALU = mybir.AluOpType
ACT = mybir.ActivationFunctionType

P = 128
PASSES = PEAKS // 512
TILES = CELLS // P
BANK = 512
GENE_BANKS = GENES // BANK

X_WORD_CHUNKS = ((0, 2), (2, 4), (4, 8), (8, 12), (12, 16))
X_SCALE_CHUNKS = ((0, 2), (2, 6), (6, 16))
V_WORD_CHUNKS = ((0, 1), (1, 3), (3, 6))
HALF = PASSES // 2
OFFSET_ROWS = COMPS // (2 * P)
BIAS_ROWS = 8
BIAS_ROW_WORDS = GENES // (2 * BIAS_ROWS)
WORD_ROWS = OFFSET_ROWS + BIAS_ROWS
DEPTH_ROW0 = 32


def tile_scatac_lsi_activity_s4_kernel(
    tc, x_words, x_scales, v_words, v_scales, w_words, w_scales, depth, offset, bias, out
):
    nc = tc.nc
    with ExitStack() as ctx:
        keep = ctx.enter_context(tc.tile_pool(name="keep", bufs=1))
        work = ctx.enter_context(tc.tile_pool(name="work", bufs=4))
        psum = ctx.enter_context(tc.psum_pool(name="psum", bufs=1))
        ctx.enter_context(tc.manual_schedule())

        def plane_tile(engine, name, passes, cols):
            plane = keep.tile([P, passes, cols], U8, name=name, align_bytes=64)
            engine.memset(plane[:].rearrange("p g n -> p (g n)").bitcast(I32), 0)
            return plane

        def load_scale_row(queue, plane, scales, r, col0, col1):
            rows = scales.bitcast(I32).rearrange("g (q r) n -> r q g n", r=4)
            queue.dma_start(out=plane[r:P:32, :, :].bitcast(I32), in_=rows[r, :, :, col0 // 4 : col1 // 4])

        x_rows = x_words.bitcast(I32).rearrange("g p n -> p g n")
        v_rows = v_words.bitcast(I32).rearrange("g p n -> p g n")

        def load_x_words(queue, chunk, g0=0, g1=PASSES):
            t0, t1 = X_WORD_CHUNKS[chunk]
            words = keep.tile([P, g1 - g0, (t1 - t0) * P * 2], U8, name="xw%d_%d" % (chunk, g0), align_bytes=64)
            queue.dma_start(out=words[:].bitcast(I32), in_=x_rows[:, g0:g1, t0 * P // 2 : t1 * P // 2])
            for g in range(g0, g1):
                xw[chunk, g] = words[:, g - g0, :]

        def load_v_words(chunk):
            g0, g1 = V_WORD_CHUNKS[chunk]
            words = keep.tile([P, g1 - g0, COMPS * 2], U8, name="vw%d" % chunk, align_bytes=64)
            nc.sync.dma_start(out=words[:].bitcast(I32), in_=v_rows[:, g0:g1, :])
            for g in range(g0, g1):
                vw[g] = words[:, g - g0, :]

        def x_plane_tile(engine, chunk):
            t0, t1 = X_SCALE_CHUNKS[chunk]
            return plane_tile(engine, "x_plane%d" % chunk, PASSES, (t1 - t0) * P)

        def load_x_scale_row(queue, chunk, r):
            t0, t1 = X_SCALE_CHUNKS[chunk]
            load_scale_row(queue, xs[chunk], x_scales, r, t0 * P, t1 * P)

        xw, xs, vw = {}, {}, {}
        ident = keep.tile([P, P], F32, name="ident")
        make_identity(nc, ident[:])
        vec_rows = keep.tile([P, 2 * P], BF16, name="vec_rows")
        nc.vector.memset(vec_rows[:], 0.0)
        v_plane = plane_tile(nc.vector, "v_plane", PASSES, COMPS)
        xs[0] = x_plane_tile(nc.vector, 0)
        xs[1] = x_plane_tile(nc.vector, 1)
        w_plane = plane_tile(nc.vector, "w_plane", 1, GENES)
        xs[2] = x_plane_tile(nc.vector, 2)

        nc.sync.dma_start(out=vec_rows[0:OFFSET_ROWS, :], in_=offset.rearrange("(r n) -> r n", n=2 * P))
        nc.sync.dma_start(out=vec_rows[DEPTH_ROW0 : DEPTH_ROW0 + TILES, 0:P], in_=depth.rearrange("(t p) -> t p", p=P))
        nc.sync.dma_start(
            out=vec_rows[OFFSET_ROWS:WORD_ROWS, 0 : 2 * BIAS_ROW_WORDS], in_=bias.rearrange("(r n) -> r n", r=BIAS_ROWS)
        )
        load_x_words(nc.scalar, 0, 0, HALF)
        for r in range(4):
            load_scale_row(nc.sync, v_plane, v_scales, r, 0, COMPS)
        ident_bf = keep.tile([P, P], BF16, name="ident_bf")
        nc.scalar.activation(out=ident_bf[:], in_=ident[:], func=ACT.Relu)
        load_v_words(0)
        for r in range(4):
            load_x_scale_row(nc.sync, 0, r)
        load_v_words(1)
        load_x_words(nc.sync, 0, HALF, PASSES)
        load_v_words(2)
        load_x_words(nc.sync, 1)
        for r in range(4):
            load_x_scale_row(nc.sync, 1, r)
        w_codes = keep.tile([P, GENES], U32, name="w_codes", align_bytes=64)
        nc.sync.dma_start(out=w_codes[:].bitcast(I32), in_=w_words[0].rearrange("p n t -> p (n t)").bitcast(I32))
        for r in range(4):
            load_scale_row(nc.sync, w_plane, w_scales, r, 0, GENES)
        load_x_words(nc.sync, 2)
        for r in range(4):
            load_x_scale_row(nc.sync, 2, r)
        load_x_words(nc.sync, 3)
        load_x_words(nc.sync, 4)

        depth_col = keep.tile([P, TILES], F32, name="depth_col")
        word_cols = keep.tile([P, WORD_ROWS], F32, name="word_cols")
        cols_ps = psum.tile([P, P], F32, name="cols_ps", tag="y", bufs=2)
        nc.tensor.transpose(cols_ps[:], vec_rows[:].bitcast(F32), ident[:])
        nc.scalar.copy(out=word_cols[:], in_=cols_ps[:, 0:WORD_ROWS])
        depth_ps = psum.tile([P, P], BF16, name="depth_ps", tag="y", bufs=2)
        nc.tensor.transpose(depth_ps[:], vec_rows[:, 0:P], ident_bf[:])
        nc.vector.tensor_copy(out=depth_col[:], in_=depth_ps[:, DEPTH_ROW0 : DEPTH_ROW0 + TILES])

        def spread(row0, row1):
            spread_ps = psum.tile([P, (row1 - row0) * P], F32, name="spread_ps", tag="a", bufs=6)
            for r in range(row0, row1):
                nc.tensor.transpose(
                    spread_ps[:, (r - row0) * P : (r - row0 + 1) * P],
                    word_cols[:, r : r + 1].to_broadcast([P, P]), ident[:],
                )
            return spread_ps

        offset_b = keep.tile([P, 2, P, 2], BF16, name="offset_b")
        bias_b = keep.tile([P, GENES], BF16, name="bias_b")
        nc.vector.tensor_copy(
            out=offset_b[:].rearrange("p u q e -> p (u q e)").bitcast(F32).rearrange("p (u q) -> p u q", u=2),
            in_=spread(0, OFFSET_ROWS)[:].rearrange("p (q u) -> p u q", u=2),
        )
        bias_words = bias_b[:].bitcast(F32).rearrange("p (r n) -> p r n", r=BIAS_ROWS)
        half = BIAS_ROWS // 2
        for h, copy in enumerate((nc.scalar.copy, nc.vector.tensor_copy)):
            rows_ps = spread(OFFSET_ROWS + h * half, OFFSET_ROWS + (h + 1) * half)
            copy(
                out=bias_words[:, h * half : (h + 1) * half, :],
                in_=rows_ps[:].rearrange("p (r n) -> p r n", r=half)[:, :, 0:BIAS_ROW_WORDS],
            )

        y_ps, z, zt, z_codes, z_scales, res, a_ps = {}, {}, {}, {}, {}, {}, {}

        def chunk_of(chunks, i):
            return [(c, i - t0) for c, (t0, t1) in enumerate(chunks) if t0 <= i < t1][0]

        def project(i, g):
            if g == 0:
                y_ps[i] = psum.tile([P, COMPS], F32, name="y", tag="y", bufs=2)
            wc, wi = chunk_of(X_WORD_CHUNKS, i)
            sc, si = chunk_of(X_SCALE_CHUNKS, i)
            nc.tensor.matmul_mx(
                out=y_ps[i][:],
                lhsT=xw[wc, g][:, wi * P * 2 : (wi + 1) * P * 2].bitcast(FP4X4),
                lhsT_scale=xs[sc][:, g, si * P : (si + 1) * P],
                rhs=vw[g].bitcast(FP4X4),
                rhs_scale=v_plane[:, g, :],
                start=(g == 0),
                stop=(g == PASSES - 1),
            )

        def normalise(i):
            z[i] = work.tile([P, 2, P, 2], BF16, name="z", tag="z")
            y_view = y_ps[i][:].rearrange("p (q u e) -> p u q e", u=2, e=2)
            for u in range(2):
                nc.vector.scalar_tensor_tensor(
                    out=z[i][:, u, :, :], in0=y_view[:, u, :, :], scalar=depth_col[:, i : i + 1],
                    in1=offset_b[:, u, :, :], op0=ALU.mult, op1=ALU.add,
                )

        def turn(t0, t1):
            n = t1 - t0
            turned = psum.tile([P, n, 2, P], F32, name="turned", tag="y", bufs=2)
            for i in range(t0, t1):
                words = z[i][:].rearrange("p u q e -> p (u q e)").bitcast(F32)
                for u in range(2):
                    nc.tensor.transpose(turned[:, i - t0, u, :], words[:, u * P : (u + 1) * P], ident[:])
            zt[t0] = work.tile([P, n * P * 4], BF16, name="zt", tag="zt", align_bytes=64)
            nc.scalar.copy(
                out=zt[t0][:].bitcast(F32).rearrange("p (i c u) -> p i c u", i=n, u=2),
                in_=turned[:].rearrange("p i u c -> p i c u"),
            )

        def quantise(t0, t1):
            n = t1 - t0
            codes = work.tile([P, n * P], U32, name="codes", tag="codes", align_bytes=64)
            scales = work.tile([P, n * P], U8, name="scales", tag="scales", align_bytes=64)
            nc.vector.quantize_mx(out=codes[:].bitcast(FP8X4), scales=scales[:], in_=zt[t0][:])
            for i in range(t0, t1):
                z_codes[i] = codes[:, (i - t0) * P : (i - t0 + 1) * P]
                z_scales[i] = scales[:, (i - t0) * P : (i - t0 + 1) * P]

        def read_out(i):
            res[i] = work.tile([P, GENES], F32, name="res", tag="res", bufs=8)
            for b in range(GENE_BANKS):
                cols = slice(b * BANK, (b + 1) * BANK)
                a_ps[i, b] = psum.tile([P, BANK], F32, name="a", tag="a", bufs=6)
                nc.tensor.matmul_mx(
                    out=a_ps[i, b][:],
                    lhsT=z_codes[i].bitcast(FP8X4),
                    lhsT_scale=z_scales[i],
                    rhs=w_codes[:, cols].bitcast(FP8X4),
                    rhs_scale=w_plane[:, 0, cols],
                    start=True,
                    stop=True,
                )

        def finish(i, b):
            rows = slice(i * P, (i + 1) * P)
            cols = slice(b * BANK, (b + 1) * BANK)
            nc.vector.tensor_tensor(out=res[i][:, cols], in0=a_ps[i, b][:], in1=bias_b[:, cols], op=ALU.add)
            nc.scalar.activation(out=res[i][:, cols], in_=res[i][:, cols], func=ACT.Relu)
            if i >= TILES - 3:
                nc.sync.dma_start(out=out[rows, cols], in_=res[i][:, cols])
            elif b == GENE_BANKS - 1:
                nc.sync.dma_start(out=out[rows, :], in_=res[i][:])

        def finish_last_bank():
            i, b = TILES - 1, GENE_BANKS - 1
            halves = [slice(c0, c0 + BANK // 2) for c0 in (0, BANK // 2)]
            last = res[i][:, b * BANK :]
            for half_cols in halves:
                nc.vector.tensor_tensor(
                    out=last[:, half_cols], in0=a_ps[i, b][:, half_cols],
                    in1=bias_b[:, b * BANK :][:, half_cols], op=ALU.add,
                )
            for half_cols in halves:
                nc.vector.tensor_scalar_max(out=last[:, half_cols], in0=last[:, half_cols], scalar1=0.0)
                nc.sync.dma_start(out=out[i * P :, b * BANK :][:, half_cols], in_=last[:, half_cols])

        def project_tile(i):
            for g in range(PASSES):
                project(i, g)
                if i == 2 and g == GENE_BANKS - 1:
                    turn(0, 2)
                    quantise(0, 2)
            normalise(i)

        def read_out_round(tiles, group, before_turn, before_quantise):
            banks = [(i, b) for i in tiles for b in range(GENE_BANKS)]
            for i in tiles:
                read_out(i)
            for i, b in banks[:before_turn]:
                finish(i, b)
            turn(*group)
            for i, b in banks[before_turn:before_quantise]:
                finish(i, b)
            quantise(*group)
            for i, b in banks[before_quantise:]:
                finish(i, b)

        for g in range(HALF):
            project(0, g)
            project(1, g)
        for i in range(2):
            for g in range(HALF, PASSES):
                project(i, g)
            normalise(i)
        for t in range(2, TILES - 4, 2):
            project_tile(t)
            project_tile(t + 1)
            read_out_round((t - 2, t - 1), (t, t + 2), 2, 4)
        project_tile(TILES - 4)
        read_out_round((TILES - 6, TILES - 5), (TILES - 4, TILES - 3), 2, 4)
        for t in range(TILES - 3, TILES):
            project_tile(t)
            read_out_round((t - 1,), (t, t + 1), 0, 2)
        read_out(TILES - 1)
        for b in range(GENE_BANKS - 1):
            finish(TILES - 1, b)
        finish_last_bank()
